import numpy as np
import ml_dtypes


def mxq(x, axis, fmt="e4m3"):
    dtype, down = {"e4m3": (ml_dtypes.float8_e4m3fn, 7), "e5m2": (ml_dtypes.float8_e5m2, 14)}[fmt]
    v = np.moveaxis(np.asarray(x, np.float32).astype(ml_dtypes.bfloat16).astype(np.float64), axis, -1)
    blocks = v.reshape(v.shape[:-1] + (-1, 32))
    amax = np.abs(blocks).max(-1, keepdims=True)
    byte = np.maximum(np.where(amax > 0, np.frexp(amax)[1] - 1 + 127, 0) - down, 1)
    scale = np.exp2(byte - 127.0)
    codes = (blocks / scale).astype(np.float32).astype(dtype).astype(np.float64)
    return np.moveaxis((codes * scale).reshape(v.shape), -1, axis)


WIDE = False


def mx_kscale(k):
    if not WIDE:
        return np.ones(k)
    levels = np.array([10, -10, 5, -5, 0])
    if k % 512:
        return np.exp2(np.random.permutation(np.resize(levels, k // 32))).repeat(32)
    a = np.empty((k // 512, 16))
    for p in range(k // 512):
        a[p, :8] = np.random.permutation(np.resize(levels, 8))
        for g in range(8):
            far = levels[np.abs(levels - a[p, g]) >= 10]
            a[p, g + 8] = far[np.random.randint(len(far))]
    return np.exp2(a.ravel()).repeat(32)


def f64(x):
    return np.asarray(x).astype(np.float64)


def striped(idx):
    return np.tile(idx.reshape(-1, 16).T, (8, 1)).astype(np.uint16)


def unstriped(offs):
    return offs[:16].T.reshape(-1).astype(np.int64)


def striped8(idx):
    return np.concatenate([v.reshape(-1, 16).T for v in idx]).astype(np.uint16)


def unstriped8(offs):
    return np.stack([offs[16 * g:16 * g + 16].T.reshape(-1) for g in range(8)]).astype(np.int64)


E2M1 = np.array([0.0, 0.5, 1.0, 1.5, 2.0, 3.0, 4.0, 6.0, -0.0, -0.5, -1.0, -1.5, -2.0, -3.0, -4.0, -6.0])


def pack_weight(w, fmt):
    k, n = w.shape
    w = f64(np.asarray(w, np.float32).astype(ml_dtypes.bfloat16)).reshape(k // 32, 32, n)
    amax = np.abs(w).max(1)
    if fmt == "e4m3":
        byte = np.frexp(amax)[1] - 1 + 127 - 7
    else:
        mant, ex = np.frexp(amax / 6.0)
        byte = np.where(mant > 0.5, ex, ex - 1) + 127
    byte = np.clip(np.where(amax > 0, byte, 1), 1, 254)
    scaled = (w * np.exp2(127.0 - byte)[:, None, :]).reshape(k, n).astype(np.float32)
    by_word = np.ascontiguousarray(scaled.reshape(k // 512, 128, 4, n).transpose(0, 1, 3, 2))
    if fmt == "e4m3":
        words = by_word.astype(ml_dtypes.float8_e4m3fn).view(np.uint8)
    else:
        c = by_word.astype(ml_dtypes.float4_e2m1fn).view(np.uint8) & 0xF
        words = (c[..., 0::2] | (c[..., 1::2] << 4)).reshape(k // 512, 128, 2 * n)
    return np.ascontiguousarray(words), np.ascontiguousarray(byte.astype(np.uint8).reshape(k // 512, 16, n))


def unpack_weight(words, scales, fmt):
    g, _, n = scales.shape
    words = np.ascontiguousarray(words).reshape(g, 128, n, -1)
    if fmt == "e4m3":
        vals = words.view(ml_dtypes.float8_e4m3fn).astype(np.float64)
    else:
        nib = np.empty((g, 128, n, 4), np.uint8)
        nib[..., 0::2] = words & 0xF
        nib[..., 1::2] = words >> 4
        vals = E2M1[nib]
    vals = vals * np.repeat(np.exp2(scales.astype(np.float64) - 127.0), 8, axis=1)[..., None]
    return vals.transpose(0, 1, 3, 2).reshape(g * 512, n)


def pack_table(v):
    words, scales = pack_weight(v, "e4m3")
    return np.concatenate([words.reshape(words.shape[0], -1), scales.reshape(scales.shape[0], -1)], axis=1)


def unpack_table(tab):
    g, t = tab.shape[0], tab.shape[1] // 528
    return unpack_weight(tab[:, :512 * t].reshape(g, 128, t, 4), tab[:, 512 * t:].reshape(g, 16, t), "e4m3")


K, M, T, S = 1024, 512, 2048, 1024


def setup_inputs():
    n = np.random.standard_normal
    s = mx_kscale(K)[:, None]
    return {
        "tab": pack_table(n((K, T)) * s),
        "w": (n((K, M)) / np.sqrt(K) / s).astype(np.float32),
        "b": (0.3 * n(512)).astype(np.float32),
        "wgo": np.repeat(np.random.uniform(0.5, 2.0, (8, S)), 16, axis=0).astype(np.float32),
        "offs": striped(np.random.permutation(T)[:S]),
        "offs2": striped8(np.stack([np.random.permutation(T)[:S] for _ in range(8)])),
    }


def reference(tab, w, b, wgo, offs, offs2):
    tab_ = unpack_table(tab)[:, unstriped(offs)]
    w_ = mxq(f64(w), 0, "e4m3")
    y = w_.T @ tab_
    place = unstriped8(offs2)[np.arange(M) % 128 // 16]
    out = np.zeros((M, T))
    out[np.arange(M)[:, None], place] = f64(wgo)[np.arange(M) % 128] * (y + f64(b)[:, None])
    return out

@@ -1,0 +1,134 @@
+import concourse.mybir as mybir
+
+FLOPS = 2 * 1024 * 512 * 1024
+
+F32 = mybir.dt.float32
+BF16 = mybir.dt.bfloat16
+I32 = mybir.dt.int32
+U32 = mybir.dt.uint32
+U16 = mybir.dt.uint16
+U8 = mybir.dt.uint8
+FP8X4 = mybir.dt.float8_e4m3fn_x4
+MULT = mybir.AluOpType.mult
+IDENTITY = mybir.ActivationFunctionType.Identity
+
+P = 128
+K, M, T, S = 1024, 512, 2048, 1024
+PASSES = K // 512
+HALF = 512
+BLOCKS = M // P
+
+
+def tile_list_tabhs_bias_kernel(tc, tab, w, b, wgo, offs, offs2, out):
+    nc = tc.nc
+    with (
+        tc.tile_pool(name="keep", bufs=1) as keep,
+        tc.psum_pool(name="psum", bufs=1) as psum,
+    ):
+        pick = keep.tile([P, S // 16], U16, name="pick")
+        place = keep.tile([P, S // 16], U16, name="place")
+        nc.sync.dma_start(pick[:], offs)
+
+        scales = keep.tile([P, T], U8, name="scales", align_bytes=64)
+        nc.vector.memset(scales[:].bitcast(I32), 0)
+        scale_rows = tab[:, 512 * T :].rearrange("a (q r c) -> q a r c", q=4, r=4)
+        for q in range(4):
+            nc.sync.dma_start(scales[32 * q : 32 * q + 8, :].bitcast(I32), scale_rows[q].bitcast(I32))
+
+        words = []
+        for a in range(PASSES):
+            words.append(keep.tile([P, T], I32, name=f"words{a}", align_bytes=64))
+
+        def load_words(a):
+            nc.sync.dma_start(words[a][:], tab[a, 0 : 512 * T].rearrange("(p x) -> p x", p=P).bitcast(I32))
+
+        w_rows = w.rearrange("(a p j) m -> a p j m", a=PASSES, j=4)
+        spans = [(0, 1), (1, 2), (2, 4)]
+        raw = [[keep.tile([P, 4, (hi - lo) * P], F32, name=f"raw{lo}{a}") for a in range(PASSES)] for lo, hi in spans]
+
+        def load_weights(i):
+            lo, hi = spans[i]
+            for a in range(PASSES):
+                nc.sync.dma_start(raw[i][a][:], w_rows[a][:, :, lo * P : hi * P])
+
+        load_words(0)
+        load_weights(0)
+        load_words(1)
+        nc.sync.dma_start(place[:], offs2)
+        bias = keep.tile([P, BLOCKS], F32, name="bias")
+        with tc.nc.allow_non_contiguous_dma(reason="one bias value a partition"):
+            nc.scalar.dma_start(bias[:], b.rearrange("(c p) -> p c", p=P))
+        weight = [keep.tile([P, HALF], F32, name=f"weight{h}") for h in range(2)]
+        nc.sync.dma_start(weight[0][:], wgo[:, 0:HALF])
+        load_weights(1)
+        nc.sync.dma_start(weight[1][:], wgo[:, HALF:S])
+        load_weights(2)
+
+        window = [keep.tile([P, T], F32, name=f"window{m}") for m in range(BLOCKS)]
+        for m in range(BLOCKS):
+            nc.gpsimd.memset(window[m][:], 0.0)
+
+        picked_scales = keep.tile([P, S], U8, name="picked_scales", align_bytes=64)
+        nc.vector.tensor_copy(picked_scales[:], scales[:].indirect(pick[:]))
+        picked = [keep.tile([P, S], U32, name=f"picked{a}", align_bytes=64) for a in range(1)]
+        nc.vector.tensor_copy(picked[0][:], words[0][:].bitcast(U32).indirect(pick[:]))
+        last = [keep.tile([P, HALF], U32, name=f"last{h}", align_bytes=64) for h in range(2)]
+        nc.vector.tensor_copy(last[0][:], words[1][:].bitcast(U32).indirect(pick[:, 0:32]))
+
+        def codes_of(a, h):
+            return picked[0][:, h * HALF : (h + 1) * HALF] if a == 0 else last[h][:]
+
+        def quantize(m):
+            grouped = keep.tile([P, PASSES, P, 4], BF16, name=f"grouped{m}", align_bytes=64)
+            for a in range(PASSES):
+                i = min(m, 2)
+                c0 = (m - spans[i][0]) * P
+                source = raw[i][a][:, :, c0 : c0 + P]
+                nc.scalar.copy(grouped[:, a], source.rearrange("p j c -> p c j"))
+            codes = keep.tile([P, PASSES * P], U32, name=f"codes{m}", align_bytes=64)
+            plane = keep.tile([P, PASSES * P], U8, name=f"plane{m}", align_bytes=64)
+            nc.vector.quantize_mx(out=codes[:].bitcast(FP8X4), scales=plane[:], in_=grouped[:].rearrange("p a c j -> p (a c j)"))
+            return codes, plane
+
+        def project(m, h, codes, plane):
+            acc = psum.tile([P, HALF], F32, name=f"acc{m}{h}")
+            for a in range(PASSES):
+                nc.tensor.matmul_mx(
+                    out=acc[:],
+                    lhsT=codes[:, a * P : (a + 1) * P].bitcast(FP8X4),
+                    lhsT_scale=plane[:, a * P : (a + 1) * P],
+                    rhs=codes_of(a, h).bitcast(FP8X4),
+                    rhs_scale=picked_scales[4 * a : P, h * HALF : (h + 1) * HALF],
+                    start=(a == 0),
+                    stop=(a == PASSES - 1),
+                )
+            y = keep.tile([P, HALF], F32, name=f"y{m}{h}")
+            nc.scalar.activation(y[:], acc[:], IDENTITY, bias=bias[:, m : m + 1])
+            return y
+
+        def put(m, h, y):
+            nc.vector.tensor_tensor(window[m][:].indirect(place[:, 32 * h : 32 * h + 32]), y[:], weight[h][:], MULT)
+
+        def store(m):
+            nc.sync.dma_start(out[m * P : (m + 1) * P, :], window[m][:])
+
+        q0 = quantize(0)
+        y00 = project(0, 0, *q0)
+        nc.vector.tensor_copy(last[1][:], words[1][:].bitcast(U32).indirect(pick[:, 32:64]))
+        y01 = project(0, 1, *q0)
+        put(0, 0, y00)
+        waiting = []
+        for m in range(1, BLOCKS):
+            q = quantize(m)
+            waiting.append([project(m, h, *q) for h in range(2)])
+            if m == 1:
+                put(0, 1, y01)
+                store(0)
+            if m == 2:
+                put(1, 0, waiting[0][0])
+        put(1, 1, waiting[0][1])
+        store(1)
+        for m in range(2, BLOCKS):
+            for h in range(2):
+                put(m, h, waiting[m - 1][h])
+            store(m)

@@ -17,6 +17,7 @@ K, M, T, S = 1024, 512, 2048, 1024
 PASSES = K // 512
 HALF = 512
 BLOCKS = M // P
+PAIR = 2 * P
 
 
 def tile_list_tabhs_bias_kernel(tc, tab, w, b, wgo, offs, offs2, out):
@@ -30,39 +31,33 @@ def tile_list_tabhs_bias_kernel(tc, tab, w, b, wgo, offs, offs2, out):
         nc.sync.dma_start(pick[:], offs)
 
         scales = keep.tile([P, T], U8, name="scales", align_bytes=64)
-        nc.vector.memset(scales[:].bitcast(I32), 0)
+        nc.gpsimd.memset(scales[:].bitcast(I32), 0)
         scale_rows = tab[:, 512 * T :].rearrange("a (q r c) -> q a r c", q=4, r=4)
         for q in range(4):
             nc.sync.dma_start(scales[32 * q : 32 * q + 8, :].bitcast(I32), scale_rows[q].bitcast(I32))
 
-        words = []
-        for a in range(PASSES):
-            words.append(keep.tile([P, T], I32, name=f"words{a}", align_bytes=64))
+        words = [keep.tile([P, T], I32, name=f"words{a}", align_bytes=64) for a in range(PASSES)]
 
         def load_words(a):
             nc.sync.dma_start(words[a][:], tab[a, 0 : 512 * T].rearrange("(p x) -> p x", p=P).bitcast(I32))
 
         w_rows = w.rearrange("(a p j) m -> a p j m", a=PASSES, j=4)
-        spans = [(0, 1), (1, 2), (2, 4)]
-        raw = [[keep.tile([P, 4, (hi - lo) * P], F32, name=f"raw{lo}{a}") for a in range(PASSES)] for lo, hi in spans]
+        raw = [[keep.tile([P, 4, PAIR], F32, name=f"raw{i}{a}", tag=f"raw{i}{a}") for a in range(PASSES)] for i in range(2)]
 
         def load_weights(i):
-            lo, hi = spans[i]
             for a in range(PASSES):
-                nc.sync.dma_start(raw[i][a][:], w_rows[a][:, :, lo * P : hi * P])
+                nc.sync.dma_start(raw[i][a][:], w_rows[a][:, :, i * PAIR : (i + 1) * PAIR])
 
         load_words(0)
         load_weights(0)
         load_words(1)
         nc.sync.dma_start(place[:], offs2)
         bias = keep.tile([P, BLOCKS], F32, name="bias")
-        with tc.nc.allow_non_contiguous_dma(reason="one bias value a partition"):
+        with nc.allow_non_contiguous_dma(reason="one bias value a partition"):
             nc.scalar.dma_start(bias[:], b.rearrange("(c p) -> p c", p=P))
-        weight = [keep.tile([P, HALF], F32, name=f"weight{h}") for h in range(2)]
+        weight = [keep.tile([P, HALF], F32, name="weight0")]
         nc.sync.dma_start(weight[0][:], wgo[:, 0:HALF])
         load_weights(1)
-        nc.sync.dma_start(weight[1][:], wgo[:, HALF:S])
-        load_weights(2)
 
         window = [keep.tile([P, T], F32, name=f"window{m}") for m in range(BLOCKS)]
         for m in range(BLOCKS):
@@ -70,33 +65,34 @@ def tile_list_tabhs_bias_kernel(tc, tab, w, b, wgo, offs, offs2, out):
 
         picked_scales = keep.tile([P, S], U8, name="picked_scales", align_bytes=64)
         nc.vector.tensor_copy(picked_scales[:], scales[:].indirect(pick[:]))
-        picked = [keep.tile([P, S], U32, name=f"picked{a}", align_bytes=64) for a in range(1)]
-        nc.vector.tensor_copy(picked[0][:], words[0][:].bitcast(U32).indirect(pick[:]))
-        last = [keep.tile([P, HALF], U32, name=f"last{h}", align_bytes=64) for h in range(2)]
-        nc.vector.tensor_copy(last[0][:], words[1][:].bitcast(U32).indirect(pick[:, 0:32]))
+        picked0 = keep.tile([P, S], U32, name="picked0", align_bytes=64)
+        nc.vector.tensor_copy(picked0[:], words[0][:].bitcast(U32).indirect(pick[:]))
+        picked1 = [keep.tile([P, HALF], U32, name=f"picked1{h}", align_bytes=64) for h in range(2)]
+        nc.vector.tensor_copy(picked1[0][:], words[1][:].bitcast(U32).indirect(pick[:, 0:32]))
 
         def codes_of(a, h):
-            return picked[0][:, h * HALF : (h + 1) * HALF] if a == 0 else last[h][:]
+            return picked0[:, h * HALF : (h + 1) * HALF] if a == 0 else picked1[h][:]
 
-        def quantize(m):
-            grouped = keep.tile([P, PASSES, P, 4], BF16, name=f"grouped{m}", align_bytes=64)
+        def quantize(i):
+            grouped = keep.tile([P, PASSES, PAIR, 4], BF16, name=f"grouped{i}", align_bytes=64)
             for a in range(PASSES):
-                i = min(m, 2)
-                c0 = (m - spans[i][0]) * P
-                source = raw[i][a][:, :, c0 : c0 + P]
-                nc.scalar.copy(grouped[:, a], source.rearrange("p j c -> p c j"))
-            codes = keep.tile([P, PASSES * P], U32, name=f"codes{m}", align_bytes=64)
-            plane = keep.tile([P, PASSES * P], U8, name=f"plane{m}", align_bytes=64)
+                nc.scalar.copy(grouped[:, a], raw[i][a][:].rearrange("p j c -> p c j"))
+            codes = keep.tile([P, PASSES * PAIR], U32, name=f"codes{i}", align_bytes=64)
+            plane = keep.tile([P, PASSES * PAIR], U8, name=f"plane{i}", align_bytes=64)
             nc.vector.quantize_mx(out=codes[:].bitcast(FP8X4), scales=plane[:], in_=grouped[:].rearrange("p a c j -> p (a c j)"))
             return codes, plane
 
-        def project(m, h, codes, plane):
+        quantized = []
+
+        def project(m, h):
+            codes, plane = quantized[m // 2]
             acc = psum.tile([P, HALF], F32, name=f"acc{m}{h}")
             for a in range(PASSES):
+                c0 = a * PAIR + (m % 2) * P
                 nc.tensor.matmul_mx(
                     out=acc[:],
-                    lhsT=codes[:, a * P : (a + 1) * P].bitcast(FP8X4),
-                    lhsT_scale=plane[:, a * P : (a + 1) * P],
+                    lhsT=codes[:, c0 : c0 + P].bitcast(FP8X4),
+                    lhsT_scale=plane[:, c0 : c0 + P],
                     rhs=codes_of(a, h).bitcast(FP8X4),
                     rhs_scale=picked_scales[4 * a : P, h * HALF : (h + 1) * HALF],
                     start=(a == 0),
@@ -109,26 +105,16 @@ def tile_list_tabhs_bias_kernel(tc, tab, w, b, wgo, offs, offs2, out):
         def put(m, h, y):
             nc.vector.tensor_tensor(window[m][:].indirect(place[:, 32 * h : 32 * h + 32]), y[:], weight[h][:], MULT)
 
-        def store(m):
-            nc.sync.dma_start(out[m * P : (m + 1) * P, :], window[m][:])
-
-        q0 = quantize(0)
-        y00 = project(0, 0, *q0)
-        nc.vector.tensor_copy(last[1][:], words[1][:].bitcast(U32).indirect(pick[:, 32:64]))
-        y01 = project(0, 1, *q0)
+        quantized.append(quantize(0))
+        y00 = project(0, 0)
+        y10 = project(1, 0)
+        nc.vector.tensor_copy(picked1[1][:], words[1][:].bitcast(U32).indirect(pick[:, 32:64]))
         put(0, 0, y00)
-        waiting = []
-        for m in range(1, BLOCKS):
-            q = quantize(m)
-            waiting.append([project(m, h, *q) for h in range(2)])
-            if m == 1:
-                put(0, 1, y01)
-                store(0)
-            if m == 2:
-                put(1, 0, waiting[0][0])
-        put(1, 1, waiting[0][1])
-        store(1)
-        for m in range(2, BLOCKS):
-            for h in range(2):
-                put(m, h, waiting[m - 1][h])
-            store(m)
+        put(1, 0, y10)
+        quantized.append(quantize(1))
+        weight.append(keep.tile([P, HALF], F32, name="weight1", tag="raw10"))
+        nc.sync.dma_start(weight[1][:], wgo[:, HALF:S])
+        for m in range(BLOCKS):
+            for h in range(1 if m < 2 else 0, 2):
+                put(m, h, project(m, h))
+            nc.sync.dma_start(out[m * P : (m + 1) * P, :], window[m][:])

@@ -24,6 +24,7 @@ def tile_list_tabhs_bias_kernel(tc, tab, w, b, wgo, offs, offs2, out):
     nc = tc.nc
     with (
         tc.tile_pool(name="keep", bufs=1) as keep,
+        tc.tile_pool(name="ring", bufs=2) as ring,
         tc.psum_pool(name="psum", bufs=1) as psum,
     ):
         pick = keep.tile([P, S // 16], U16, name="pick")
@@ -31,10 +32,8 @@ def tile_list_tabhs_bias_kernel(tc, tab, w, b, wgo, offs, offs2, out):
         nc.sync.dma_start(pick[:], offs)
 
         scales = keep.tile([P, T], U8, name="scales", align_bytes=64)
-        nc.gpsimd.memset(scales[:].bitcast(I32), 0)
+        nc.vector.memset(scales[:].bitcast(I32), 0)
         scale_rows = tab[:, 512 * T :].rearrange("a (q r c) -> q a r c", q=4, r=4)
-        for q in range(4):
-            nc.sync.dma_start(scales[32 * q : 32 * q + 8, :].bitcast(I32), scale_rows[q].bitcast(I32))
 
         words = [keep.tile([P, T], I32, name=f"words{a}", align_bytes=64) for a in range(PASSES)]
 
@@ -49,14 +48,16 @@ def tile_list_tabhs_bias_kernel(tc, tab, w, b, wgo, offs, offs2, out):
                 nc.sync.dma_start(raw[i][a][:], w_rows[a][:, :, i * PAIR : (i + 1) * PAIR])
 
         load_words(0)
+        for q in range(4):
+            nc.sync.dma_start(scales[32 * q : 32 * q + 8, :].bitcast(I32), scale_rows[q].bitcast(I32))
         load_weights(0)
         load_words(1)
         nc.sync.dma_start(place[:], offs2)
-        bias = keep.tile([P, BLOCKS], F32, name="bias")
-        with nc.allow_non_contiguous_dma(reason="one bias value a partition"):
-            nc.scalar.dma_start(bias[:], b.rearrange("(c p) -> p c", p=P))
         weight = [keep.tile([P, HALF], F32, name="weight0")]
         nc.sync.dma_start(weight[0][:], wgo[:, 0:HALF])
+        bias = keep.tile([P, BLOCKS], F32, name="bias")
+        with nc.allow_non_contiguous_dma(reason="one bias value a partition"):
+            nc.sync.dma_start(bias[:], b.rearrange("(c p) -> p c", p=P))
         load_weights(1)
 
         window = [keep.tile([P, T], F32, name=f"window{m}") for m in range(BLOCKS)]
@@ -64,31 +65,31 @@ def tile_list_tabhs_bias_kernel(tc, tab, w, b, wgo, offs, offs2, out):
             nc.gpsimd.memset(window[m][:], 0.0)
 
         picked_scales = keep.tile([P, S], U8, name="picked_scales", align_bytes=64)
-        nc.vector.tensor_copy(picked_scales[:], scales[:].indirect(pick[:]))
         picked0 = keep.tile([P, S], U32, name="picked0", align_bytes=64)
         nc.vector.tensor_copy(picked0[:], words[0][:].bitcast(U32).indirect(pick[:]))
+        nc.vector.tensor_copy(picked_scales[:], scales[:].indirect(pick[:]))
         picked1 = [keep.tile([P, HALF], U32, name=f"picked1{h}", align_bytes=64) for h in range(2)]
-        nc.vector.tensor_copy(picked1[0][:], words[1][:].bitcast(U32).indirect(pick[:, 0:32]))
 
         def codes_of(a, h):
             return picked0[:, h * HALF : (h + 1) * HALF] if a == 0 else picked1[h][:]
 
-        def quantize(i):
-            grouped = keep.tile([P, PASSES, PAIR, 4], BF16, name=f"grouped{i}", align_bytes=64)
+        def quantize(m):
+            grouped = keep.tile([P, PASSES, P, 4], BF16, name=f"grouped{m}", align_bytes=64)
             for a in range(PASSES):
-                nc.scalar.copy(grouped[:, a], raw[i][a][:].rearrange("p j c -> p c j"))
-            codes = keep.tile([P, PASSES * PAIR], U32, name=f"codes{i}", align_bytes=64)
-            plane = keep.tile([P, PASSES * PAIR], U8, name=f"plane{i}", align_bytes=64)
+                c0 = (m % 2) * P
+                nc.scalar.copy(grouped[:, a], raw[m // 2][a][:, :, c0 : c0 + P].rearrange("p j c -> p c j"))
+            codes = keep.tile([P, PASSES * P], U32, name=f"codes{m}", align_bytes=64)
+            plane = keep.tile([P, PASSES * P], U8, name=f"plane{m}", align_bytes=64)
             nc.vector.quantize_mx(out=codes[:].bitcast(FP8X4), scales=plane[:], in_=grouped[:].rearrange("p a c j -> p (a c j)"))
             return codes, plane
 
         quantized = []
 
         def project(m, h):
-            codes, plane = quantized[m // 2]
+            codes, plane = quantized[m]
             acc = psum.tile([P, HALF], F32, name=f"acc{m}{h}")
             for a in range(PASSES):
-                c0 = a * PAIR + (m % 2) * P
+                c0 = a * P
                 nc.tensor.matmul_mx(
                     out=acc[:],
                     lhsT=codes[:, c0 : c0 + P].bitcast(FP8X4),
@@ -98,7 +99,7 @@ def tile_list_tabhs_bias_kernel(tc, tab, w, b, wgo, offs, offs2, out):
                     start=(a == 0),
                     stop=(a == PASSES - 1),
                 )
-            y = keep.tile([P, HALF], F32, name=f"y{m}{h}")
+            y = ring.tile([P, HALF], F32, name="y")
             nc.scalar.activation(y[:], acc[:], IDENTITY, bias=bias[:, m : m + 1])
             return y
 
@@ -106,15 +107,22 @@ def tile_list_tabhs_bias_kernel(tc, tab, w, b, wgo, offs, offs2, out):
             nc.vector.tensor_tensor(window[m][:].indirect(place[:, 32 * h : 32 * h + 32]), y[:], weight[h][:], MULT)
 
         quantized.append(quantize(0))
+        nc.vector.tensor_copy(picked1[0][:], words[1][:].bitcast(U32).indirect(pick[:, 0:32]))
         y00 = project(0, 0)
+        quantized.append(quantize(1))
         y10 = project(1, 0)
         nc.vector.tensor_copy(picked1[1][:], words[1][:].bitcast(U32).indirect(pick[:, 32:64]))
         put(0, 0, y00)
         put(1, 0, y10)
-        quantized.append(quantize(1))
+        quantized.append(quantize(2))
+        quantized.append(quantize(3))
         weight.append(keep.tile([P, HALF], F32, name="weight1", tag="raw10"))
         nc.sync.dma_start(weight[1][:], wgo[:, HALF:S])
-        for m in range(BLOCKS):
-            for h in range(1 if m < 2 else 0, 2):
+        for m in range(2):
+            put(m, 1, project(m, 1))
+            nc.sync.dma_start(out[m * P : (m + 1) * P, :], window[m][:])
+        for h in range(2):
+            for m in range(2, BLOCKS):
                 put(m, h, project(m, h))
+        for m in range(2, BLOCKS):
             nc.sync.dma_start(out[m * P : (m + 1) * P, :], window[m][:])

@@ -1,4 +1,5 @@
 import concourse.mybir as mybir
+from concourse.masks import make_identity
 
 FLOPS = 2 * 1024 * 512 * 1024
 
@@ -10,6 +11,7 @@ U16 = mybir.dt.uint16
 U8 = mybir.dt.uint8
 FP8X4 = mybir.dt.float8_e4m3fn_x4
 MULT = mybir.AluOpType.mult
+ADD = mybir.AluOpType.add
 IDENTITY = mybir.ActivationFunctionType.Identity
 
 P = 128
@@ -43,51 +45,66 @@ def tile_list_tabhs_bias_kernel(tc, tab, w, b, wgo, offs, offs2, out):
         w_rows = w.rearrange("(a p j) m -> a p j m", a=PASSES, j=4)
         raw = [[keep.tile([P, 4, PAIR], F32, name=f"raw{i}{a}", tag=f"raw{i}{a}") for a in range(PASSES)] for i in range(2)]
 
-        def load_weights(i):
-            for a in range(PASSES):
-                nc.sync.dma_start(raw[i][a][:], w_rows[a][:, :, i * PAIR : (i + 1) * PAIR])
+        def load_weights(i, a):
+            nc.sync.dma_start(raw[i][a][:], w_rows[a][:, :, i * PAIR : (i + 1) * PAIR])
 
-        load_words(0)
+        nc.sync.dma_start(place[:], offs2)
+        load_weights(0, 0)
         for q in range(4):
             nc.sync.dma_start(scales[32 * q : 32 * q + 8, :].bitcast(I32), scale_rows[q].bitcast(I32))
-        load_weights(0)
+        load_words(0)
+        load_weights(0, 1)
         load_words(1)
-        nc.sync.dma_start(place[:], offs2)
         weight = [keep.tile([P, HALF], F32, name="weight0")]
         nc.sync.dma_start(weight[0][:], wgo[:, 0:HALF])
+        load_weights(1, 0)
+        load_weights(1, 1)
+
+        bias_rows = keep.tile([P, P], F32, name="bias_rows")
+        nc.gpsimd.memset(bias_rows[:], 0.0)
+        nc.scalar.dma_start(bias_rows[0:BLOCKS, :], b.rearrange("(c p) -> c p", p=P))
+        identity = keep.tile([P, P], F32, name="identity")
+        make_identity(nc, identity[:])
+        turned = psum.tile([P, P], F32, name="turned", tag="acc31")
+        nc.tensor.transpose(turned[:], bias_rows[:], identity[:])
         bias = keep.tile([P, BLOCKS], F32, name="bias")
-        with nc.allow_non_contiguous_dma(reason="one bias value a partition"):
-            nc.sync.dma_start(bias[:], b.rearrange("(c p) -> p c", p=P))
-        load_weights(1)
+        nc.scalar.copy(bias[:], turned[:, 0:BLOCKS])
 
         window = [keep.tile([P, T], F32, name=f"window{m}") for m in range(BLOCKS)]
-        for m in range(BLOCKS):
+        nc.vector.memset(window[BLOCKS - 1][:], 0.0)
+        for m in range(BLOCKS - 1):
             nc.gpsimd.memset(window[m][:], 0.0)
 
         picked_scales = keep.tile([P, S], U8, name="picked_scales", align_bytes=64)
         picked0 = keep.tile([P, S], U32, name="picked0", align_bytes=64)
-        nc.vector.tensor_copy(picked0[:], words[0][:].bitcast(U32).indirect(pick[:]))
         nc.vector.tensor_copy(picked_scales[:], scales[:].indirect(pick[:]))
+        nc.vector.tensor_copy(picked0[:], words[0][:].bitcast(U32).indirect(pick[:]))
         picked1 = [keep.tile([P, HALF], U32, name=f"picked1{h}", align_bytes=64) for h in range(2)]
 
         def codes_of(a, h):
             return picked0[:, h * HALF : (h + 1) * HALF] if a == 0 else picked1[h][:]
 
-        def quantize(m):
-            grouped = keep.tile([P, PASSES, P, 4], BF16, name=f"grouped{m}", align_bytes=64)
+        grouped = {}
+
+        def interleave(i):
+            for m in (2 * i, 2 * i + 1):
+                grouped[m] = keep.tile([P, PASSES, P, 4], BF16, name=f"grouped{m}", align_bytes=64)
             for a in range(PASSES):
-                c0 = (m % 2) * P
-                nc.scalar.copy(grouped[:, a], raw[m // 2][a][:, :, c0 : c0 + P].rearrange("p j c -> p c j"))
+                for m in (2 * i, 2 * i + 1):
+                    c0 = (m % 2) * P
+                    nc.scalar.copy(grouped[m][:, a], raw[i][a][:, :, c0 : c0 + P].rearrange("p j c -> p c j"))
+
+        def quantize(m):
             codes = keep.tile([P, PASSES * P], U32, name=f"codes{m}", align_bytes=64)
             plane = keep.tile([P, PASSES * P], U8, name=f"plane{m}", align_bytes=64)
-            nc.vector.quantize_mx(out=codes[:].bitcast(FP8X4), scales=plane[:], in_=grouped[:].rearrange("p a c j -> p (a c j)"))
+            nc.vector.quantize_mx(out=codes[:].bitcast(FP8X4), scales=plane[:], in_=grouped[m][:].rearrange("p a c j -> p (a c j)"))
             return codes, plane
 
         quantized = []
 
         def project(m, h):
             codes, plane = quantized[m]
-            acc = psum.tile([P, HALF], F32, name=f"acc{m}{h}")
+            acc = psum.tile([P, HALF], F32, name=f"acc{m}{h}", tag=f"acc{m}{h}")
             for a in range(PASSES):
                 c0 = a * P
                 nc.tensor.matmul_mx(
@@ -100,12 +117,16 @@ def tile_list_tabhs_bias_kernel(tc, tab, w, b, wgo, offs, offs2, out):
                     stop=(a == PASSES - 1),
                 )
             y = ring.tile([P, HALF], F32, name="y")
-            nc.scalar.activation(y[:], acc[:], IDENTITY, bias=bias[:, m : m + 1])
+            if m == 0 and h == 0:
+                nc.vector.tensor_scalar(y[:], acc[:], bias[:, m : m + 1], None, op0=ADD)
+            else:
+                nc.scalar.activation(y[:], acc[:], IDENTITY, bias=bias[:, m : m + 1])
             return y
 
         def put(m, h, y):
             nc.vector.tensor_tensor(window[m][:].indirect(place[:, 32 * h : 32 * h + 32]), y[:], weight[h][:], MULT)
 
+        interleave(0)
         quantized.append(quantize(0))
         nc.vector.tensor_copy(picked1[0][:], words[1][:].bitcast(U32).indirect(pick[:, 0:32]))
         y00 = project(0, 0)
@@ -114,6 +135,7 @@ def tile_list_tabhs_bias_kernel(tc, tab, w, b, wgo, offs, offs2, out):
         nc.vector.tensor_copy(picked1[1][:], words[1][:].bitcast(U32).indirect(pick[:, 32:64]))
         put(0, 0, y00)
         put(1, 0, y10)
+        interleave(1)
         quantized.append(quantize(2))
         quantized.append(quantize(3))
         weight.append(keep.tile([P, HALF], F32, name="weight1", tag="raw10"))

import concourse.mybir as mybir
from concourse.masks import make_identity

FLOPS = 2 * 1024 * 512 * 1024

F32 = mybir.dt.float32
BF16 = mybir.dt.bfloat16
I32 = mybir.dt.int32
U32 = mybir.dt.uint32
U16 = mybir.dt.uint16
U8 = mybir.dt.uint8
FP8X4 = mybir.dt.float8_e4m3fn_x4
MULT = mybir.AluOpType.mult
ADD = mybir.AluOpType.add
IDENTITY = mybir.ActivationFunctionType.Identity

P = 128
K, M, T, S = 1024, 512, 2048, 1024
PASSES = K // 512
HALF = 512
BLOCKS = M // P
PAIR = 2 * P


def tile_list_tabhs_bias_kernel(tc, tab, w, b, wgo, offs, offs2, out):
    nc = tc.nc
    with (
        tc.tile_pool(name="keep", bufs=1) as keep,
        tc.tile_pool(name="ring", bufs=2) as ring,
        tc.psum_pool(name="psum", bufs=1) as psum,
    ):
        pick = keep.tile([P, S // 16], U16, name="pick")
        place = keep.tile([P, S // 16], U16, name="place")
        nc.sync.dma_start(pick[:], offs)

        scales = keep.tile([P, T], U8, name="scales", align_bytes=64)
        nc.vector.memset(scales[:].bitcast(I32), 0)
        scale_rows = tab[:, 512 * T :].rearrange("a (q r c) -> q a r c", q=4, r=4)

        words = [keep.tile([P, T], I32, name=f"words{a}", align_bytes=64) for a in range(PASSES)]

        def load_words(a):
            nc.sync.dma_start(words[a][:], tab[a, 0 : 512 * T].rearrange("(p x) -> p x", p=P).bitcast(I32))

        w_rows = w.rearrange("(a p j) m -> a p j m", a=PASSES, j=4)
        raw = [[keep.tile([P, 4, PAIR], F32, name=f"raw{i}{a}", tag=f"raw{i}{a}") for a in range(PASSES)] for i in range(2)]

        def load_weights(i, a):
            nc.sync.dma_start(raw[i][a][:], w_rows[a][:, :, i * PAIR : (i + 1) * PAIR])

        nc.sync.dma_start(place[:], offs2)
        load_weights(0, 0)
        for q in range(4):
            nc.sync.dma_start(scales[32 * q : 32 * q + 8, :].bitcast(I32), scale_rows[q].bitcast(I32))
        load_words(0)
        load_weights(0, 1)
        load_words(1)
        weight = [keep.tile([P, HALF], F32, name="weight0")]
        nc.sync.dma_start(weight[0][:], wgo[:, 0:HALF])
        load_weights(1, 0)
        load_weights(1, 1)

        bias_rows = keep.tile([P, P], F32, name="bias_rows")
        nc.gpsimd.memset(bias_rows[:], 0.0)
        nc.scalar.dma_start(bias_rows[0:BLOCKS, :], b.rearrange("(c p) -> c p", p=P))
        identity = keep.tile([P, P], F32, name="identity")
        make_identity(nc, identity[:])
        turned = psum.tile([P, P], F32, name="turned", tag="acc31")
        nc.tensor.transpose(turned[:], bias_rows[:], identity[:])
        bias = keep.tile([P, BLOCKS], F32, name="bias")
        nc.scalar.copy(bias[:], turned[:, 0:BLOCKS])

        window = [keep.tile([P, T], F32, name=f"window{m}") for m in range(BLOCKS)]
        nc.vector.memset(window[BLOCKS - 1][:], 0.0)
        for m in range(BLOCKS - 1):
            nc.gpsimd.memset(window[m][:], 0.0)

        picked_scales = keep.tile([P, S], U8, name="picked_scales", align_bytes=64)
        picked0 = keep.tile([P, S], U32, name="picked0", align_bytes=64)
        nc.vector.tensor_copy(picked_scales[:], scales[:].indirect(pick[:]))
        nc.vector.tensor_copy(picked0[:], words[0][:].bitcast(U32).indirect(pick[:]))
        picked1 = [keep.tile([P, HALF], U32, name=f"picked1{h}", align_bytes=64) for h in range(2)]

        def codes_of(a, h):
            return picked0[:, h * HALF : (h + 1) * HALF] if a == 0 else picked1[h][:]

        grouped = {}

        def interleave(i):
            for m in (2 * i, 2 * i + 1):
                grouped[m] = keep.tile([P, PASSES, P, 4], BF16, name=f"grouped{m}", align_bytes=64)
            for a in range(PASSES):
                for m in (2 * i, 2 * i + 1):
                    c0 = (m % 2) * P
                    nc.scalar.copy(grouped[m][:, a], raw[i][a][:, :, c0 : c0 + P].rearrange("p j c -> p c j"))

        def quantize(m):
            codes = keep.tile([P, PASSES * P], U32, name=f"codes{m}", align_bytes=64)
            plane = keep.tile([P, PASSES * P], U8, name=f"plane{m}", align_bytes=64)
            nc.vector.quantize_mx(out=codes[:].bitcast(FP8X4), scales=plane[:], in_=grouped[m][:].rearrange("p a c j -> p (a c j)"))
            return codes, plane

        quantized = []

        def project(m, h):
            codes, plane = quantized[m]
            acc = psum.tile([P, HALF], F32, name=f"acc{m}{h}", tag=f"acc{m}{h}")
            for a in range(PASSES):
                c0 = a * P
                nc.tensor.matmul_mx(
                    out=acc[:],
                    lhsT=codes[:, c0 : c0 + P].bitcast(FP8X4),
                    lhsT_scale=plane[:, c0 : c0 + P],
                    rhs=codes_of(a, h).bitcast(FP8X4),
                    rhs_scale=picked_scales[4 * a : P, h * HALF : (h + 1) * HALF],
                    start=(a == 0),
                    stop=(a == PASSES - 1),
                )
            y = ring.tile([P, HALF], F32, name="y")
            if m == 0 and h == 0:
                nc.vector.tensor_scalar(y[:], acc[:], bias[:, m : m + 1], None, op0=ADD)
            else:
                nc.scalar.activation(y[:], acc[:], IDENTITY, bias=bias[:, m : m + 1])
            return y

        def put(m, h, y):
            nc.vector.tensor_tensor(window[m][:].indirect(place[:, 32 * h : 32 * h + 32]), y[:], weight[h][:], MULT)

        interleave(0)
        quantized.append(quantize(0))
        nc.vector.tensor_copy(picked1[0][:], words[1][:].bitcast(U32).indirect(pick[:, 0:32]))
        y00 = project(0, 0)
        quantized.append(quantize(1))
        y10 = project(1, 0)
        nc.vector.tensor_copy(picked1[1][:], words[1][:].bitcast(U32).indirect(pick[:, 32:64]))
        put(0, 0, y00)
        put(1, 0, y10)
        interleave(1)
        quantized.append(quantize(2))
        quantized.append(quantize(3))
        weight.append(keep.tile([P, HALF], F32, name="weight1", tag="raw10"))
        nc.sync.dma_start(weight[1][:], wgo[:, HALF:S])
        for m in range(2):
            put(m, 1, project(m, 1))
            nc.sync.dma_start(out[m * P : (m + 1) * P, :], window[m][:])
        for h in range(2):
            for m in range(2, BLOCKS):
                put(m, h, project(m, h))
        for m in range(2, BLOCKS):
            nc.sync.dma_start(out[m * P : (m + 1) * P, :], window[m][:])
